import numpy as np
import ml_dtypes


def mxq(x, axis, fmt="e4m3"):
    dtype, down = {"e4m3": (ml_dtypes.float8_e4m3fn, 7), "e5m2": (ml_dtypes.float8_e5m2, 14)}[fmt]
    v = np.moveaxis(np.asarray(x, np.float32).astype(ml_dtypes.bfloat16).astype(np.float64), axis, -1)
    blocks = v.reshape(v.shape[:-1] + (-1, 32))
    amax = np.abs(blocks).max(-1, keepdims=True)
    byte = np.maximum(np.where(amax > 0, np.frexp(amax)[1] - 1 + 127, 0) - down, 1)
    scale = np.exp2(byte - 127.0)
    codes = (blocks / scale).astype(np.float32).astype(dtype).astype(np.float64)
    return np.moveaxis((codes * scale).reshape(v.shape), -1, axis)


WIDE = False


def mx_kscale(k):
    if not WIDE:
        return np.ones(k)
    levels = np.array([10, -10, 5, -5, 0])
    if k % 512:
        return np.exp2(np.random.permutation(np.resize(levels, k // 32))).repeat(32)
    a = np.empty((k // 512, 16))
    for p in range(k // 512):
        a[p, :8] = np.random.permutation(np.resize(levels, 8))
        for g in range(8):
            far = levels[np.abs(levels - a[p, g]) >= 10]
            a[p, g + 8] = far[np.random.randint(len(far))]
    return np.exp2(a.ravel()).repeat(32)


def f64(x):
    return np.asarray(x).astype(np.float64)


def striped(idx):
    return np.tile(idx.reshape(-1, 16).T, (8, 1)).astype(np.uint16)


def unstriped(offs):
    return offs[:16].T.reshape(-1).astype(np.int64)


def pack_weight(w):
    k, n = w.shape
    w = f64(np.asarray(w, np.float32).astype(ml_dtypes.bfloat16)).reshape(k // 32, 32, n)
    amax = np.abs(w).max(1)
    byte = np.clip(np.where(amax > 0, np.frexp(amax)[1] - 1 + 127 - 7, 1), 1, 254)
    scaled = (w * np.exp2(127.0 - byte)[:, None, :]).reshape(k, n).astype(np.float32)
    words = np.ascontiguousarray(scaled.reshape(k // 512, 128, 4, n).transpose(0, 1, 3, 2)).astype(ml_dtypes.float8_e4m3fn).view(np.uint8)
    return words, np.ascontiguousarray(byte.astype(np.uint8).reshape(k // 512, 16, n))


def unpack_weight(words, scales):
    g, p, n, _ = words.shape
    vals = np.ascontiguousarray(words).view(ml_dtypes.float8_e4m3fn).astype(np.float64) * np.repeat(np.exp2(scales.astype(np.float64) - 127.0), 8, axis=1)[..., None]
    return vals.transpose(0, 1, 3, 2).reshape(g * 512, n)


def planes(y):
    n, m = y.shape
    v = y.astype(np.float32).astype(ml_dtypes.bfloat16).astype(np.float64).reshape(n // 32, 32, m)
    top = np.abs(v).max(1)
    byte = np.clip(np.where(top > 0, np.frexp(top)[1] - 1 + 127 - 7, 1), 1, 254)
    codes = (v * np.exp2(127.0 - byte)[:, None, :]).reshape(n, m).astype(np.float32).astype(ml_dtypes.float8_e4m3fn).view(np.uint8)
    words = codes.reshape(n // 512, 128, 4, m).transpose(0, 1, 3, 2)
    return np.ascontiguousarray(words), np.ascontiguousarray(byte.astype(np.uint8).reshape(n // 512, 16, m))


K, T, S, N, H, W, G, U = 512, 2048, 512, 512, 512, 2048, 1024, 1024


def setup_inputs():
    n = np.random.standard_normal
    s = mx_kscale(K)[:, None]
    u = mx_kscale(H)
    packed_xT = pack_weight(n((K, T)) * s)
    packed_eT = pack_weight(n((K, W)) * s)
    packed_dT = pack_weight(n((K, G)) * s)
    return {
        "x_words": packed_xT[0],
        "x_scales": packed_xT[1],
        "w1": (n((K, N)) / np.sqrt(K) / s).astype(np.float32),
        "e_words": packed_eT[0],
        "e_scales": packed_eT[1],
        "w2": (n((K, N)) / np.sqrt(K) / s).astype(np.float32),
        "d_words": packed_dT[0],
        "d_scales": packed_dT[1],
        "w3": (n((K, N)) / np.sqrt(K) / s).astype(np.float32),
        "unit": (np.random.uniform(0.6, 1.4, (H, 1)) * u[:, None]).astype(np.float32),
        "w4": (n((H, N)) / np.sqrt(H) / u[:, None]).astype(np.float32),
        "offs": striped(np.random.permutation(T)[:S]),
        "gra": striped(np.random.permutation(W)[:S]),
        "grb": striped(np.random.permutation(G)[:S]),
        "sc_": striped(np.random.permutation(np.concatenate([np.arange(S), np.random.randint(0, S, U - S)]))),
        "ra": striped(np.random.permutation(np.concatenate([np.arange(S), np.random.randint(0, S, U - S)]))),
        "rb": striped(np.random.permutation(np.concatenate([np.arange(S), np.random.randint(0, S, U - S)]))),
    }


def reference(x_words, x_scales, w1, e_words, e_scales, w2, d_words, d_scales, w3, unit, w4, offs, gra, grb, sc_, ra, rb):
    xq = unpack_weight(x_words, x_scales)[:, unstriped(offs)]
    y = mxq(f64(w1), 0, "e4m3").T @ xq
    ys1 = y[:, unstriped(sc_)]
    e_gra = unpack_weight(e_words, e_scales)[:, unstriped(gra)]
    ye = mxq(f64(w2), 0, "e4m3").T @ e_gra
    ea = ye[:, unstriped(ra)]
    d_grb = unpack_weight(d_words, d_scales)[:, unstriped(grb)]
    yd = mxq(f64(w3), 0, "e4m3").T @ d_grb
    db = yd[:, unstriped(rb)]
    clash = np.minimum(ea, db)
    mol = ys1 + ea + db - (1.3 * clash)
    hid = f64(unit) * (mol * ys1)
    out_0 = mxq(f64(w4), 0, "e4m3").T @ mxq(hid, 0, "e4m3")
    return (out_0,) + planes(out_0)

@@ -1,0 +1,233 @@
+from contextlib import ExitStack
+
+import concourse.mybir as mybir
+
+F32 = mybir.dt.float32
+BF16 = mybir.dt.bfloat16
+I32 = mybir.dt.int32
+U32 = mybir.dt.uint32
+U16 = mybir.dt.uint16
+U8 = mybir.dt.uint8
+FP8X4 = mybir.dt.float8_e4m3fn_x4
+ALU = mybir.AluOpType
+COPY = mybir.ActivationFunctionType.Copy
+
+P = 128
+PACK = 4
+K = 512
+PICKED = 512
+MOLECULES = 1024
+SPARE = 8
+CHUNKS = ((0, 256), (256, 256), (512, 256), (768, 256))
+BANK = 512
+
+FLOPS = 2 * K * K * (3 * PICKED + MOLECULES)
+
+
+def tile_picked_yscafld_mul_po_kernel(
+    tc, x_words, x_scales, w1, e_words, e_scales, w2, d_words, d_scales, w3, unit, w4,
+    offs, gra, grb, sc_, ra, rb, out_0, out_1, out_2,
+):
+    nc = tc.nc
+    with ExitStack() as ctx:
+        keep = ctx.enter_context(tc.tile_pool(name="keep", bufs=1))
+        psum = ctx.enter_context(tc.psum_pool(name="psum", bufs=1))
+
+        def load_list(name, src):
+            t = keep.tile(list(src.shape), U16, name=name)
+            nc.sync.dma_start(t[:], src)
+            return t
+
+        def load_weight(name, w):
+            raw = keep.tile([P, PACK, K], F32, name=name + "_raw", align_bytes=64)
+            nc.sync.dma_start(raw[:], w.rearrange("(p j) n -> p j n", j=PACK))
+            return raw
+
+        def load_words(name, words):
+            cols = words.shape[2]
+            t = keep.tile([P, cols], I32, name=name + "_words", align_bytes=64)
+            nc.sync.dma_start(t[:], words[0].rearrange("p n r -> p (n r)").bitcast(I32))
+            return t
+
+        def clear_scales(name, scales):
+            t = keep.tile([P, scales.shape[2]], U8, name=name + "_scales", align_bytes=64)
+            nc.gpsimd.memset(t[:].bitcast(I32), 0)
+            return t
+
+        def load_scales(queue, t, scales):
+            for q in range(4):
+                queue.dma_start(t[32 * q : 32 * q + 4, :].bitcast(I32), scales[0, 4 * q : 4 * q + 4, :].bitcast(I32))
+
+        d_sc = clear_scales("d", d_scales)
+        e_sc = clear_scales("e", e_scales)
+        x_sc = clear_scales("x", x_scales)
+        load_scales(nc.scalar, d_sc, d_scales)
+
+        grb_t = load_list("grb", grb)
+        rb_t = load_list("rb", rb)
+        u = keep.tile([P, PACK], F32, name="u")
+        nc.sync.dma_start(u[:], unit.rearrange("(p t) o -> p (t o)", t=PACK))
+        d_wd = load_words("d", d_words)
+        w3_raw = load_weight("w3", w3)
+        gra_t = load_list("gra", gra)
+        e_wd = load_words("e", e_words)
+        load_scales(nc.sync, e_sc, e_scales)
+        w2_raw = load_weight("w2", w2)
+        ra_t = load_list("ra", ra)
+        offs_t = load_list("offs", offs)
+        x_wd = load_words("x", x_words)
+        load_scales(nc.sync, x_sc, x_scales)
+        w1_raw = load_weight("w1", w1)
+        sc_t = load_list("sc", sc_)
+        w4_raw = load_weight("w4", w4)
+
+        tables = {}
+        for name in ("yd", "ye", "y"):
+            tables[name] = [keep.tile([P, PICKED + SPARE], F32, name="%s%d" % (name, t)) for t in range(PACK)]
+            for t in range(PACK):
+                nc.vector.memset(tables[name][t][:, PICKED:], 0.0)
+
+        sign_u = keep.tile([P, PACK], F32, name="sign_u")
+        abs_u = keep.tile([P, PACK], F32, name="abs_u")
+        neg_abs_u = keep.tile([P, PACK], F32, name="neg_abs_u")
+        nc.vector.tensor_scalar(sign_u[:], u[:], 0.0, 2.0, ALU.is_ge, ALU.mult)
+        nc.vector.tensor_scalar(sign_u[:], sign_u[:], 1.0, -1.0, ALU.mult, ALU.add)
+        nc.vector.tensor_tensor(abs_u[:], u[:], sign_u[:], ALU.mult)
+        nc.vector.tensor_scalar(neg_abs_u[:], abs_u[:], -1.0, 0.0, ALU.mult, ALU.add)
+
+        def round_weight(name, raw, scalar_share):
+            grouped = keep.tile([P, PACK * P * PACK], BF16, name=name + "_bf", align_bytes=64)
+            dst = grouped[:].rearrange("p (t m j) -> p m j t", t=PACK, j=PACK)
+            src = raw[:].rearrange("p j (m t) -> p m j t", t=PACK)
+            cut = P - scalar_share
+            if cut > 0:
+                nc.vector.tensor_copy(dst[:, :cut], src[:, :cut])
+            if cut < P:
+                nc.scalar.copy(dst[:, cut:], src[:, cut:])
+            return grouped
+
+        def quantize(name, grouped):
+            width = grouped.shape[1] // PACK
+            codes = keep.tile([P, width], U32, name=name + "_codes", align_bytes=64)
+            scales = keep.tile([P, width], U8, name=name + "_qs", align_bytes=64)
+            nc.vector.quantize_mx(out=codes[:].bitcast(FP8X4), scales=scales[:], in_=grouped[:])
+            return codes, scales
+
+        def pick(name, src, lst, dtype):
+            got = keep.tile([P, PICKED], dtype, name=name, align_bytes=64)
+            nc.vector.tensor_copy(got[:], src.indirect(lst[:]))
+            return got
+
+        banks = [0]
+
+        def new_bank():
+            b = banks[0] % 8
+            banks[0] = banks[0] + 1
+            return psum.tile([P, BANK], F32, name="bank%d" % b)
+
+        def first_product(name, wq, words, scales, factor):
+            for t in range(PACK):
+                acc = new_bank()
+                cols = slice(t * P, (t + 1) * P)
+                nc.tensor.matmul_mx(out=acc[:], lhsT=wq[0][:, cols].bitcast(FP8X4), lhsT_scale=wq[1][:, cols],
+                                    rhs=words[:].bitcast(FP8X4), rhs_scale=scales[:], start=True, stop=True)
+                nc.scalar.activation(tables[name][t][:, :PICKED], acc[:], COPY, scale=factor[:, t : t + 1])
+
+        fetched = {}
+
+        def fetch(name, c, lst, engine):
+            r0, n = CHUNKS[c]
+            if c not in fetched:
+                fetched[c] = keep.tile([P, 3, PACK, n], F32, name="fetched_c%d" % c, tag=("even", "w1_bf")[c % 2], align_bytes=64)
+            got = fetched[c][:, ("yd", "ye", "y").index(name)]
+            for t in range(PACK):
+                window = tables[name][t][:].indirect(lst[:, r0 // 16 : (r0 + n) // 16])
+                if engine[t] == "V":
+                    nc.vector.tensor_copy(got[:, t, :], window)
+                else:
+                    nc.scalar.activation(got[:, t, :], window, COPY)
+            return got
+
+        def side_part(c, a, nb):
+            n = CHUNKS[c][1]
+            work = keep.tile([P, PACK, n], F32, name="work_c%d" % c, tag="work")
+            halves = [slice(0, 2), slice(2, 4)]
+            for h in halves:
+                nc.vector.tensor_tensor(work[:, h, :], a[:, h, :], nb[:, h, :], ALU.add)
+            for h in halves:
+                nc.vector.scalar_tensor_tensor(work[:, h, :], work[:, h, :], -0.3, work[:, h, :], ALU.mult, ALU.max)
+            for h in halves:
+                nc.vector.scalar_tensor_tensor(work[:, h, :], nb[:, h, :], -0.7, work[:, h, :], ALU.mult, ALU.add)
+            return work
+
+        def hidden(c, work, s):
+            n = CHUNKS[c][1]
+            for t in range(PACK):
+                nc.vector.scalar_tensor_tensor(work[:, t, :], s[:, t, :], u[:, t : t + 1], work[:, t, :], ALU.mult, ALU.add)
+            hid = keep.tile([P, n * PACK], BF16, name="hid_c%d" % c, tag="stage", align_bytes=64)
+            dst = hid[:].rearrange("p (c e t) -> p c t e", t=PACK, e=4)
+            nc.vector.tensor_tensor(dst, work[:].rearrange("p t (c e) -> p c t e", e=4),
+                                    s.rearrange("p t (c e) -> p c t e", e=4), ALU.mult)
+            return hid
+
+        out_codes = keep.tile([P, MOLECULES], U32, name="out_codes", align_bytes=64)
+        out_scales = keep.tile([P, MOLECULES], U8, name="out_scales", align_bytes=64)
+        out_rows = out_0.rearrange("(p t) r -> p t r", t=PACK)
+        out_words = out_1[0].rearrange("p n r -> p (n r)").bitcast(I32)
+
+        def last_product(c, hq, w4q):
+            r0, n = CHUNKS[c]
+            res = keep.tile([P, PACK, n], F32, name="res_c%d" % c)
+            per_bank = BANK // n
+            for t0 in range(0, PACK, per_bank):
+                acc = new_bank()
+                for t in range(t0, t0 + per_bank):
+                    cols = slice(t * P, (t + 1) * P)
+                    nc.tensor.matmul_mx(out=acc[:, (t - t0) * n : (t - t0 + 1) * n], lhsT=w4q[0][:, cols].bitcast(FP8X4),
+                                        lhsT_scale=w4q[1][:, cols], rhs=hq[0][:].bitcast(FP8X4), rhs_scale=hq[1][:],
+                                        start=True, stop=True)
+                nc.scalar.copy(res[:, t0 : t0 + per_bank, :].rearrange("p t n -> p (t n)"), acc[:])
+            nc.sync.dma_start(out_rows[:, :, r0 : r0 + n], res[:])
+            return res
+
+        def planes(c, res, engine):
+            r0, n = CHUNKS[c]
+            rounded = keep.tile([P, n * PACK], BF16, name="rounded_c%d" % c, tag="stage", align_bytes=64)
+            round_copy = nc.vector.tensor_copy if engine == "V" else nc.scalar.copy
+            round_copy(rounded[:].rearrange("p (c e t) -> p c t e", t=PACK, e=4), res[:].rearrange("p t (c e) -> p c t e", e=4))
+            nc.vector.quantize_mx(out=out_codes[:, r0 : r0 + n].bitcast(FP8X4), scales=out_scales[:, r0 : r0 + n], in_=rounded[:])
+            nc.sync.dma_start(out_words[:, r0 : r0 + n], out_codes[:, r0 : r0 + n].bitcast(I32))
+
+        last = len(CHUNKS) - 1
+        d_w = pick("d_pw", d_wd[:].bitcast(U32), grb_t, U32)
+        d_s = pick("d_ps", d_sc[:], grb_t, U8)
+        w3q = quantize("w3", round_weight("w3", w3_raw, 48))
+        first_product("yd", w3q, d_w, d_s, neg_abs_u)
+        e_w = pick("e_pw", e_wd[:].bitcast(U32), gra_t, U32)
+        e_s = pick("e_ps", e_sc[:], gra_t, U8)
+        w2q = quantize("w2", round_weight("w2", w2_raw, 0))
+        nb = fetch("yd", 0, rb_t, ("SSSS","SSSS","SSSS","SSSS","SSSS")[0])
+        first_product("ye", w2q, e_w, e_s, abs_u)
+        x_w = pick("x_pw", x_wd[:].bitcast(U32), offs_t, U32)
+        x_s = pick("x_ps", x_sc[:], offs_t, U8)
+        w1q = quantize("w1", round_weight("w1", w1_raw, 0))
+        a = fetch("ye", 0, ra_t, ("SSSS", "SSSS", "SSSS", "SSSS")[0])
+        first_product("y", w1q, x_w, x_s, sign_u)
+        work = side_part(0, a, nb)
+        w4q = quantize("w4", round_weight("w4", w4_raw, 0))
+        res = None
+        for c in range(len(CHUNKS)):
+            s = fetch("y", c, sc_t, ("VVSS", "VSSS", "VSSS", "SSSS")[c])
+            if c < last:
+                nb_next = fetch("yd", c + 1, rb_t, ("SSSS","SSSS","SSSS","SSSS","SSSS")[c + 1])
+                a_next = fetch("ye", c + 1, ra_t, ("SSSS", "SSSS", "SSSS", "SSSS")[c + 1])
+            hq = quantize("hid%d" % c, hidden(c, work, s))
+            if res is not None:
+                planes(c - 1, res, "VVVVV"[c - 1])
+            res = last_product(c, hq, w4q)
+            if c < last:
+                work = side_part(c + 1, a_next, nb_next)
+        planes(last, res, "V")
+        for q in range(4):
+            eng = nc.sync if q % 2 == 0 else nc.scalar
+            eng.dma_start(out_2[0, 4 * q : 4 * q + 4, :].bitcast(I32), out_scales[32 * q : 32 * q + 4, :].bitcast(I32))

@@ -18,8 +18,11 @@ K = 512
 PICKED = 512
 MOLECULES = 1024
 SPARE = 8
-CHUNKS = ((0, 256), (256, 256), (512, 256), (768, 256))
+CHUNKS = ((0, 512), (512, 256), (768, 256))
 BANK = 512
+PIECES = ((0, 0, 512), (1, 512, 256), (2, 768, 256))
+HOME = {("yd", 0, 1): "w1_raw", ("sides", 1): "ye_c00", ("y", 1): "yd_c00", ("sides", 2): "ye_c01", ("y", 2): "s_c0", ("rounded", 0): "w1_bf", ("rounded", 1): "s_c0"}
+BY_VECTOR = (("yd", 0, 2), ("yd", 0, 3))
 
 FLOPS = 2 * K * K * (3 * PICKED + MOLECULES)
 
@@ -61,18 +64,19 @@ def tile_picked_yscafld_mul_po_kernel(
         d_sc = clear_scales("d", d_scales)
         e_sc = clear_scales("e", e_scales)
         x_sc = clear_scales("x", x_scales)
-        load_scales(nc.scalar, d_sc, d_scales)
-
         grb_t = load_list("grb", grb)
-        rb_t = load_list("rb", rb)
+        d_wd = load_words("d", d_words)
+        load_scales(nc.sync, d_sc, d_scales)
+        w3_raw = keep.tile([P, PACK, K], F32, name="w3_raw", align_bytes=64)
+        for half in (slice(K // 2, K), slice(0, K // 2)):
+            nc.sync.dma_start(w3_raw[:, :, half], w3.rearrange("(p j) n -> p j n", j=PACK)[:, :, half])
         u = keep.tile([P, PACK], F32, name="u")
         nc.sync.dma_start(u[:], unit.rearrange("(p t) o -> p (t o)", t=PACK))
-        d_wd = load_words("d", d_words)
-        w3_raw = load_weight("w3", w3)
         gra_t = load_list("gra", gra)
-        e_wd = load_words("e", e_words)
-        load_scales(nc.sync, e_sc, e_scales)
         w2_raw = load_weight("w2", w2)
+        rb_t = load_list("rb", rb)
+        load_scales(nc.sync, e_sc, e_scales)
+        e_wd = load_words("e", e_words)
         ra_t = load_list("ra", ra)
         offs_t = load_list("offs", offs)
         x_wd = load_words("x", x_words)
@@ -95,10 +99,13 @@ def tile_picked_yscafld_mul_po_kernel(
         nc.vector.tensor_tensor(abs_u[:], u[:], sign_u[:], ALU.mult)
         nc.vector.tensor_scalar(neg_abs_u[:], abs_u[:], -1.0, 0.0, ALU.mult, ALU.add)
 
-        def round_weight(name, raw, scalar_share):
+        def round_weight(name, raw, scalar_share, by_pool):
             grouped = keep.tile([P, PACK * P * PACK], BF16, name=name + "_bf", align_bytes=64)
             dst = grouped[:].rearrange("p (t m j) -> p m j t", t=PACK, j=PACK)
             src = raw[:].rearrange("p j (m t) -> p m j t", t=PACK)
+            if by_pool:
+                nc.gpsimd.tensor_scalar(dst, src, 1.0, 0.0, ALU.mult, ALU.add)
+                return grouped
             cut = P - scalar_share
             if cut > 0:
                 nc.vector.tensor_copy(dst[:, :cut], src[:, :cut])
@@ -133,41 +140,60 @@ def tile_picked_yscafld_mul_po_kernel(
                                     rhs=words[:].bitcast(FP8X4), rhs_scale=scales[:], start=True, stop=True)
                 nc.scalar.activation(tables[name][t][:, :PICKED], acc[:], COPY, scale=factor[:, t : t + 1])
 
+        lists = {"yd": rb_t, "ye": ra_t, "y": sc_t}
         fetched = {}
 
-        def fetch(name, c, lst, engine):
+        def fetch(name, c, h):
             r0, n = CHUNKS[c]
-            if c not in fetched:
-                fetched[c] = keep.tile([P, 3, PACK, n], F32, name="fetched_c%d" % c, tag=("even", "w1_bf")[c % 2], align_bytes=64)
-            got = fetched[c][:, ("yd", "ye", "y").index(name)]
+            if ("sides", c) in HOME and (name, c, h) not in HOME:
+                if c not in fetched:
+                    fetched[c] = keep.tile([P, 4, 2, n], F32, name="sides_c%d" % c, tag=HOME["sides", c], align_bytes=64)
+                got = fetched[c][:, 2 * h + (name == "ye")]
+            else:
+                got = keep.tile([P, 2, n], F32, name="%s_c%d%d" % (name, c, h),
+                                tag=HOME.get((name, c, h), "%s_c%d%d" % (name, c, h)), align_bytes=64)[:]
+            for t in (2 * h, 2 * h + 1):
+                window = tables[name][t][:].indirect(lists[name][:, r0 // 16 : (r0 + n) // 16])
+                if (name, c, t) in BY_VECTOR:
+                    nc.vector.tensor_copy(got[:, t % 2, :], window)
+                else:
+                    nc.scalar.activation(got[:, t % 2, :], window, COPY)
+            fetched[name, c, h] = got
+
+        def fetch_scaffold(c):
+            r0, n = CHUNKS[c]
+            got = keep.tile([P, PACK, n], F32, name="s_c%d" % c, tag=HOME.get(("y", c), "s_c%d" % c), align_bytes=64)
             for t in range(PACK):
-                window = tables[name][t][:].indirect(lst[:, r0 // 16 : (r0 + n) // 16])
-                if engine[t] == "V":
+                window = tables["y"][t][:].indirect(sc_t[:, r0 // 16 : (r0 + n) // 16])
+                if ("y", c, t) in BY_VECTOR:
                     nc.vector.tensor_copy(got[:, t, :], window)
                 else:
                     nc.scalar.activation(got[:, t, :], window, COPY)
             return got
 
-        def side_part(c, a, nb):
-            n = CHUNKS[c][1]
-            work = keep.tile([P, PACK, n], F32, name="work_c%d" % c, tag="work")
-            halves = [slice(0, 2), slice(2, 4)]
-            for h in halves:
-                nc.vector.tensor_tensor(work[:, h, :], a[:, h, :], nb[:, h, :], ALU.add)
-            for h in halves:
-                nc.vector.scalar_tensor_tensor(work[:, h, :], work[:, h, :], -0.3, work[:, h, :], ALU.mult, ALU.max)
-            for h in halves:
-                nc.vector.scalar_tensor_tensor(work[:, h, :], nb[:, h, :], -0.7, work[:, h, :], ALU.mult, ALU.add)
+        def flat(ap):
+            return ap.rearrange("p t n -> p (t n)")
+
+        def side_part(c):
+            work = keep.tile([P, PACK, CHUNKS[c][1]], F32, name="work_c%d" % c, tag="w1_bf", align_bytes=64)
+            parts = [(flat(work[:, 2 * h : 2 * h + 2, :]), flat(fetched["ye", c, h]), flat(fetched["yd", c, h])) for h in range(2)]
+            for w, a, nb in parts:
+                nc.vector.tensor_tensor(w, a, nb, ALU.add)
+                nc.vector.scalar_tensor_tensor(w, w, -0.3, w, ALU.mult, ALU.max)
+                nc.vector.scalar_tensor_tensor(w, nb, -0.7, w, ALU.mult, ALU.add)
             return work
 
-        def hidden(c, work, s):
-            n = CHUNKS[c][1]
+        def add_scaffold(work, s):
             for t in range(PACK):
                 nc.vector.scalar_tensor_tensor(work[:, t, :], s[:, t, :], u[:, t : t + 1], work[:, t, :], ALU.mult, ALU.add)
-            hid = keep.tile([P, n * PACK], BF16, name="hid_c%d" % c, tag="stage", align_bytes=64)
-            dst = hid[:].rearrange("p (c e t) -> p c t e", t=PACK, e=4)
-            nc.vector.tensor_tensor(dst, work[:].rearrange("p t (c e) -> p c t e", e=4),
-                                    s.rearrange("p t (c e) -> p c t e", e=4), ALU.mult)
+
+        def hidden(i, work, s):
+            c, r0, n = PIECES[i]
+            cols = slice(r0 - CHUNKS[c][0], r0 - CHUNKS[c][0] + n)
+            hid = keep.tile([P, n * PACK], BF16, name="hid_%d" % i, align_bytes=64)
+            nc.vector.tensor_tensor(hid[:].rearrange("p (c e t) -> p c t e", t=PACK, e=4),
+                                    work[:, :, cols].rearrange("p t (c e) -> p c t e", e=4),
+                                    s[:, :, cols].rearrange("p t (c e) -> p c t e", e=4), ALU.mult)
             return hid
 
         out_codes = keep.tile([P, MOLECULES], U32, name="out_codes", align_bytes=64)
@@ -175,9 +201,9 @@ def tile_picked_yscafld_mul_po_kernel(
         out_rows = out_0.rearrange("(p t) r -> p t r", t=PACK)
         out_words = out_1[0].rearrange("p n r -> p (n r)").bitcast(I32)
 
-        def last_product(c, hq, w4q):
-            r0, n = CHUNKS[c]
-            res = keep.tile([P, PACK, n], F32, name="res_c%d" % c)
+        def last_product(i, hq, w4q, engines):
+            r0, n = PIECES[i][1:]
+            res = keep.tile([P, PACK, n], F32, name="res_%d" % i)
             per_bank = BANK // n
             for t0 in range(0, PACK, per_bank):
                 acc = new_bank()
@@ -186,48 +212,55 @@ def tile_picked_yscafld_mul_po_kernel(
                     nc.tensor.matmul_mx(out=acc[:, (t - t0) * n : (t - t0 + 1) * n], lhsT=w4q[0][:, cols].bitcast(FP8X4),
                                         lhsT_scale=w4q[1][:, cols], rhs=hq[0][:].bitcast(FP8X4), rhs_scale=hq[1][:],
                                         start=True, stop=True)
-                nc.scalar.copy(res[:, t0 : t0 + per_bank, :].rearrange("p t n -> p (t n)"), acc[:])
+                out_copy = nc.vector.tensor_copy if engines[t0 // per_bank] == "V" else nc.scalar.copy
+                out_copy(flat(res[:, t0 : t0 + per_bank, :]), acc[:])
             nc.sync.dma_start(out_rows[:, :, r0 : r0 + n], res[:])
             return res
 
-        def planes(c, res, engine):
-            r0, n = CHUNKS[c]
-            rounded = keep.tile([P, n * PACK], BF16, name="rounded_c%d" % c, tag="stage", align_bytes=64)
+        def planes(i, res, engine):
+            r0, n = PIECES[i][1:]
+            rounded = keep.tile([P, n * PACK], BF16, name="rounded_%d" % i, tag=HOME.get(("rounded", i), "rounded_%d" % i), align_bytes=64)
             round_copy = nc.vector.tensor_copy if engine == "V" else nc.scalar.copy
             round_copy(rounded[:].rearrange("p (c e t) -> p c t e", t=PACK, e=4), res[:].rearrange("p t (c e) -> p c t e", e=4))
             nc.vector.quantize_mx(out=out_codes[:, r0 : r0 + n].bitcast(FP8X4), scales=out_scales[:, r0 : r0 + n], in_=rounded[:])
             nc.sync.dma_start(out_words[:, r0 : r0 + n], out_codes[:, r0 : r0 + n].bitcast(I32))
 
-        last = len(CHUNKS) - 1
         d_w = pick("d_pw", d_wd[:].bitcast(U32), grb_t, U32)
         d_s = pick("d_ps", d_sc[:], grb_t, U8)
-        w3q = quantize("w3", round_weight("w3", w3_raw, 48))
+        w3q = quantize("w3", round_weight("w3", w3_raw, 64, False))
         first_product("yd", w3q, d_w, d_s, neg_abs_u)
-        e_w = pick("e_pw", e_wd[:].bitcast(U32), gra_t, U32)
         e_s = pick("e_ps", e_sc[:], gra_t, U8)
-        w2q = quantize("w2", round_weight("w2", w2_raw, 0))
-        nb = fetch("yd", 0, rb_t, ("SSSS","SSSS","SSSS","SSSS","SSSS")[0])
+        w2_bf = round_weight("w2", w2_raw, 0, False)
+        e_w = pick("e_pw", e_wd[:].bitcast(U32), gra_t, U32)
+        w2q = quantize("w2", w2_bf)
         first_product("ye", w2q, e_w, e_s, abs_u)
         x_w = pick("x_pw", x_wd[:].bitcast(U32), offs_t, U32)
         x_s = pick("x_ps", x_sc[:], offs_t, U8)
-        w1q = quantize("w1", round_weight("w1", w1_raw, 0))
-        a = fetch("ye", 0, ra_t, ("SSSS", "SSSS", "SSSS", "SSSS")[0])
+        w1_bf = round_weight("w1", w1_raw, 0, False)
+        w1q = quantize("w1", w1_bf)
+        for h in range(2):
+            fetch("yd", 0, h)
+            fetch("ye", 0, h)
         first_product("y", w1q, x_w, x_s, sign_u)
-        work = side_part(0, a, nb)
-        w4q = quantize("w4", round_weight("w4", w4_raw, 0))
-        res = None
+        w4q = quantize("w4", round_weight("w4", w4_raw, 0, False))
+        work = side_part(0)
+        waiting = []
         for c in range(len(CHUNKS)):
-            s = fetch("y", c, sc_t, ("VVSS", "VSSS", "VSSS", "SSSS")[c])
-            if c < last:
-                nb_next = fetch("yd", c + 1, rb_t, ("SSSS","SSSS","SSSS","SSSS","SSSS")[c + 1])
-                a_next = fetch("ye", c + 1, ra_t, ("SSSS", "SSSS", "SSSS", "SSSS")[c + 1])
-            hq = quantize("hid%d" % c, hidden(c, work, s))
-            if res is not None:
-                planes(c - 1, res, "VVVVV"[c - 1])
-            res = last_product(c, hq, w4q)
-            if c < last:
-                work = side_part(c + 1, a_next, nb_next)
-        planes(last, res, "V")
+            s = fetch_scaffold(c)
+            if c + 1 < len(CHUNKS):
+                for h in range(2):
+                    fetch("yd", c + 1, h)
+                    fetch("ye", c + 1, h)
+            add_scaffold(work, s)
+            done = []
+            for i in range(len(PIECES)):
+                if PIECES[i][0] == c:
+                    done.append((i, last_product(i, quantize("hid%d" % i, hidden(i, work, s)), w4q, ("SSSS", "SS", "SS", "SS")[i])))
+            waiting = waiting + done
+            if c + 1 < len(CHUNKS):
+                work = side_part(c + 1)
+        for i, res in waiting:
+            planes(i, res, "VVV"[i])
         for q in range(4):
             eng = nc.sync if q % 2 == 0 else nc.scalar
             eng.dma_start(out_2[0, 4 * q : 4 * q + 4, :].bitcast(I32), out_scales[32 * q : 32 * q + 4, :].bitcast(I32))

@@ -21,7 +21,7 @@ SPARE = 8
 CHUNKS = ((0, 512), (512, 256), (768, 256))
 BANK = 512
 PIECES = ((0, 0, 512), (1, 512, 256), (2, 768, 256))
-HOME = {("yd", 0, 1): "w1_raw", ("sides", 1): "ye_c00", ("y", 1): "yd_c00", ("sides", 2): "ye_c01", ("y", 2): "s_c0", ("rounded", 0): "w1_bf", ("rounded", 1): "s_c0"}
+HOME = {("yd", 0, 1): "e_words", ("sides", 1): "yd_c00", ("y", 1): "ye_c00", ("sides", 2): "ye_c01", ("y", 2): "s_c0", ("rounded", 0): "w1_bf", ("rounded", 1): "s_c0"}
 BY_VECTOR = (("yd", 0, 2), ("yd", 0, 3))
 
 FLOPS = 2 * K * K * (3 * PICKED + MOLECULES)
@@ -57,30 +57,32 @@ def tile_picked_yscafld_mul_po_kernel(
             nc.gpsimd.memset(t[:].bitcast(I32), 0)
             return t
 
-        def load_scales(queue, t, scales):
-            for q in range(4):
-                queue.dma_start(t[32 * q : 32 * q + 4, :].bitcast(I32), scales[0, 4 * q : 4 * q + 4, :].bitcast(I32))
+        def load_scales(queue, t, scales, first):
+            for r in range(4):
+                queue.dma_start(t[first + r : P : 32, :].bitcast(I32), scales[0, r:16:4, :].bitcast(I32))
 
         d_sc = clear_scales("d", d_scales)
         e_sc = clear_scales("e", e_scales)
         x_sc = clear_scales("x", x_scales)
         grb_t = load_list("grb", grb)
         d_wd = load_words("d", d_words)
-        load_scales(nc.sync, d_sc, d_scales)
+        load_scales(nc.sync, d_sc, d_scales, 0)
         w3_raw = keep.tile([P, PACK, K], F32, name="w3_raw", align_bytes=64)
         for half in (slice(K // 2, K), slice(0, K // 2)):
             nc.sync.dma_start(w3_raw[:, :, half], w3.rearrange("(p j) n -> p j n", j=PACK)[:, :, half])
         u = keep.tile([P, PACK], F32, name="u")
         nc.sync.dma_start(u[:], unit.rearrange("(p t) o -> p (t o)", t=PACK))
         gra_t = load_list("gra", gra)
-        w2_raw = load_weight("w2", w2)
+        w2_raw = keep.tile([P, PACK, K], F32, name="w2_raw", align_bytes=64)
+        for half in (slice(K // 2, K), slice(0, K // 2)):
+            nc.sync.dma_start(w2_raw[:, :, half], w2.rearrange("(p j) n -> p j n", j=PACK)[:, :, half])
         rb_t = load_list("rb", rb)
-        load_scales(nc.sync, e_sc, e_scales)
+        load_scales(nc.sync, e_sc, e_scales, 4)
         e_wd = load_words("e", e_words)
         ra_t = load_list("ra", ra)
         offs_t = load_list("offs", offs)
         x_wd = load_words("x", x_words)
-        load_scales(nc.sync, x_sc, x_scales)
+        load_scales(nc.sync, x_sc, x_scales, 8)
         w1_raw = load_weight("w1", w1)
         sc_t = load_list("sc", sc_)
         w4_raw = load_weight("w4", w4)
@@ -101,16 +103,17 @@ def tile_picked_yscafld_mul_po_kernel(
 
         def round_weight(name, raw, scalar_share, by_pool):
             grouped = keep.tile([P, PACK * P * PACK], BF16, name=name + "_bf", align_bytes=64)
-            dst = grouped[:].rearrange("p (t m j) -> p m j t", t=PACK, j=PACK)
-            src = raw[:].rearrange("p j (m t) -> p m j t", t=PACK)
+            dst = grouped[:].rearrange("p (h e m j) -> p h m j e", h=2, e=2, j=PACK)
+            src = raw[:].rearrange("p j (m h e) -> p h m j e", h=2, e=2)
             if by_pool:
                 nc.gpsimd.tensor_scalar(dst, src, 1.0, 0.0, ALU.mult, ALU.add)
                 return grouped
             cut = P - scalar_share
-            if cut > 0:
-                nc.vector.tensor_copy(dst[:, :cut], src[:, :cut])
             if cut < P:
-                nc.scalar.copy(dst[:, cut:], src[:, cut:])
+                nc.scalar.copy(grouped[:].rearrange("p (t m j) -> p m j t", t=PACK, j=PACK)[:, cut:],
+                               raw[:].rearrange("p j (m t) -> p m j t", t=PACK)[:, cut:])
+            if cut > 0:
+                nc.vector.tensor_copy(dst[:, :, :cut], src[:, :, :cut])
             return grouped
 
         def quantize(name, grouped):
@@ -137,7 +140,7 @@ def tile_picked_yscafld_mul_po_kernel(
                 acc = new_bank()
                 cols = slice(t * P, (t + 1) * P)
                 nc.tensor.matmul_mx(out=acc[:], lhsT=wq[0][:, cols].bitcast(FP8X4), lhsT_scale=wq[1][:, cols],
-                                    rhs=words[:].bitcast(FP8X4), rhs_scale=scales[:], start=True, stop=True)
+                                    rhs=words[:].bitcast(FP8X4), rhs_scale=scales, start=True, stop=True)
                 nc.scalar.activation(tables[name][t][:, :PICKED], acc[:], COPY, scale=factor[:, t : t + 1])
 
         lists = {"yd": rb_t, "ye": ra_t, "y": sc_t}
@@ -175,12 +178,14 @@ def tile_picked_yscafld_mul_po_kernel(
             return ap.rearrange("p t n -> p (t n)")
 
         def side_part(c):
-            work = keep.tile([P, PACK, CHUNKS[c][1]], F32, name="work_c%d" % c, tag="w1_bf", align_bytes=64)
+            pair = keep.tile([P, 2, PACK, CHUNKS[c][1]], F32, name="work_c%d" % c, tag="w1_bf", align_bytes=64)
+            work, other = pair[:, 0], pair[:, 1]
             parts = [(flat(work[:, 2 * h : 2 * h + 2, :]), flat(fetched["ye", c, h]), flat(fetched["yd", c, h])) for h in range(2)]
-            for w, a, nb in parts:
-                nc.vector.tensor_tensor(w, a, nb, ALU.add)
-                nc.vector.scalar_tensor_tensor(w, w, -0.3, w, ALU.mult, ALU.max)
-                nc.vector.scalar_tensor_tensor(w, nb, -0.7, w, ALU.mult, ALU.add)
+            for h, (w, a, nb) in enumerate(parts):
+                o = flat(other[:, 2 * h : 2 * h + 2, :])
+                nc.vector.scalar_tensor_tensor(w, nb, 0.3, a, ALU.mult, ALU.add)
+                nc.vector.scalar_tensor_tensor(o, a, 0.3, nb, ALU.mult, ALU.add)
+                nc.vector.scalar_tensor_tensor(w, o, -1.0, w, ALU.mult, ALU.max)
             return work
 
         def add_scaffold(work, s):
@@ -191,9 +196,9 @@ def tile_picked_yscafld_mul_po_kernel(
             c, r0, n = PIECES[i]
             cols = slice(r0 - CHUNKS[c][0], r0 - CHUNKS[c][0] + n)
             hid = keep.tile([P, n * PACK], BF16, name="hid_%d" % i, align_bytes=64)
-            nc.vector.tensor_tensor(hid[:].rearrange("p (c e t) -> p c t e", t=PACK, e=4),
-                                    work[:, :, cols].rearrange("p t (c e) -> p c t e", e=4),
-                                    s[:, :, cols].rearrange("p t (c e) -> p c t e", e=4), ALU.mult)
+            nc.vector.tensor_tensor(hid[:].rearrange("p (c e t) -> p c t e", t=PACK, e=2),
+                                    work[:, :, cols].rearrange("p t (c e) -> p c t e", e=2),
+                                    s[:, :, cols].rearrange("p t (c e) -> p c t e", e=2), ALU.mult)
             return hid
 
         out_codes = keep.tile([P, MOLECULES], U32, name="out_codes", align_bytes=64)
@@ -214,26 +219,26 @@ def tile_picked_yscafld_mul_po_kernel(
                                         start=True, stop=True)
                 out_copy = nc.vector.tensor_copy if engines[t0 // per_bank] == "V" else nc.scalar.copy
                 out_copy(flat(res[:, t0 : t0 + per_bank, :]), acc[:])
-            nc.sync.dma_start(out_rows[:, :, r0 : r0 + n], res[:])
+                nc.sync.dma_start(out_rows[:, t0 : t0 + per_bank, r0 : r0 + n], res[:, t0 : t0 + per_bank, :])
             return res
 
         def planes(i, res, engine):
             r0, n = PIECES[i][1:]
             rounded = keep.tile([P, n * PACK], BF16, name="rounded_%d" % i, tag=HOME.get(("rounded", i), "rounded_%d" % i), align_bytes=64)
             round_copy = nc.vector.tensor_copy if engine == "V" else nc.scalar.copy
-            round_copy(rounded[:].rearrange("p (c e t) -> p c t e", t=PACK, e=4), res[:].rearrange("p t (c e) -> p c t e", e=4))
+            round_copy(rounded[:].rearrange("p (c e t) -> p c t e", t=PACK, e=2), res[:].rearrange("p t (c e) -> p c t e", e=2))
             nc.vector.quantize_mx(out=out_codes[:, r0 : r0 + n].bitcast(FP8X4), scales=out_scales[:, r0 : r0 + n], in_=rounded[:])
             nc.sync.dma_start(out_words[:, r0 : r0 + n], out_codes[:, r0 : r0 + n].bitcast(I32))
 
         d_w = pick("d_pw", d_wd[:].bitcast(U32), grb_t, U32)
         d_s = pick("d_ps", d_sc[:], grb_t, U8)
         w3q = quantize("w3", round_weight("w3", w3_raw, 64, False))
-        first_product("yd", w3q, d_w, d_s, neg_abs_u)
+        first_product("yd", w3q, d_w, d_s[:], neg_abs_u)
         e_s = pick("e_ps", e_sc[:], gra_t, U8)
-        w2_bf = round_weight("w2", w2_raw, 0, False)
+        w2_bf = round_weight("w2", w2_raw, 64, False)
         e_w = pick("e_pw", e_wd[:].bitcast(U32), gra_t, U32)
         w2q = quantize("w2", w2_bf)
-        first_product("ye", w2q, e_w, e_s, abs_u)
+        first_product("ye", w2q, e_w, e_s[4:P, :], abs_u)
         x_w = pick("x_pw", x_wd[:].bitcast(U32), offs_t, U32)
         x_s = pick("x_ps", x_sc[:], offs_t, U8)
         w1_bf = round_weight("w1", w1_raw, 0, False)
@@ -241,7 +246,7 @@ def tile_picked_yscafld_mul_po_kernel(
         for h in range(2):
             fetch("yd", 0, h)
             fetch("ye", 0, h)
-        first_product("y", w1q, x_w, x_s, sign_u)
+        first_product("y", w1q, x_w, x_s[8:P, :], sign_u)
         w4q = quantize("w4", round_weight("w4", w4_raw, 0, False))
         work = side_part(0)
         waiting = []
@@ -261,6 +266,6 @@ def tile_picked_yscafld_mul_po_kernel(
                 work = side_part(c + 1)
         for i, res in waiting:
             planes(i, res, "VVV"[i])
-        for q in range(4):
-            eng = nc.sync if q % 2 == 0 else nc.scalar
-            eng.dma_start(out_2[0, 4 * q : 4 * q + 4, :].bitcast(I32), out_scales[32 * q : 32 * q + 4, :].bitcast(I32))
+        for r in range(4):
+            eng = nc.sync if r % 2 == 0 else nc.scalar
+            eng.dma_start(out_2[0, r:16:4, :].bitcast(I32), out_scales[r:P:32, :].bitcast(I32))

from contextlib import ExitStack

import concourse.mybir as mybir

F32 = mybir.dt.float32
BF16 = mybir.dt.bfloat16
I32 = mybir.dt.int32
U32 = mybir.dt.uint32
U16 = mybir.dt.uint16
U8 = mybir.dt.uint8
FP8X4 = mybir.dt.float8_e4m3fn_x4
ALU = mybir.AluOpType
COPY = mybir.ActivationFunctionType.Copy

P = 128
PACK = 4
K = 512
PICKED = 512
MOLECULES = 1024
SPARE = 8
CHUNKS = ((0, 512), (512, 256), (768, 256))
BANK = 512
PIECES = ((0, 0, 512), (1, 512, 256), (2, 768, 256))
HOME = {("yd", 0, 1): "e_words", ("sides", 1): "yd_c00", ("y", 1): "ye_c00", ("sides", 2): "ye_c01", ("y", 2): "s_c0", ("rounded", 0): "w1_bf", ("rounded", 1): "s_c0"}
BY_VECTOR = (("yd", 0, 2), ("yd", 0, 3))

FLOPS = 2 * K * K * (3 * PICKED + MOLECULES)


def tile_picked_yscafld_mul_po_kernel(
    tc, x_words, x_scales, w1, e_words, e_scales, w2, d_words, d_scales, w3, unit, w4,
    offs, gra, grb, sc_, ra, rb, out_0, out_1, out_2,
):
    nc = tc.nc
    with ExitStack() as ctx:
        keep = ctx.enter_context(tc.tile_pool(name="keep", bufs=1))
        psum = ctx.enter_context(tc.psum_pool(name="psum", bufs=1))

        def load_list(name, src):
            t = keep.tile(list(src.shape), U16, name=name)
            nc.sync.dma_start(t[:], src)
            return t

        def load_weight(name, w):
            raw = keep.tile([P, PACK, K], F32, name=name + "_raw", align_bytes=64)
            nc.sync.dma_start(raw[:], w.rearrange("(p j) n -> p j n", j=PACK))
            return raw

        def load_words(name, words):
            cols = words.shape[2]
            t = keep.tile([P, cols], I32, name=name + "_words", align_bytes=64)
            nc.sync.dma_start(t[:], words[0].rearrange("p n r -> p (n r)").bitcast(I32))
            return t

        def clear_scales(name, scales):
            t = keep.tile([P, scales.shape[2]], U8, name=name + "_scales", align_bytes=64)
            nc.gpsimd.memset(t[:].bitcast(I32), 0)
            return t

        def load_scales(queue, t, scales, first):
            for r in range(4):
                queue.dma_start(t[first + r : P : 32, :].bitcast(I32), scales[0, r:16:4, :].bitcast(I32))

        d_sc = clear_scales("d", d_scales)
        e_sc = clear_scales("e", e_scales)
        x_sc = clear_scales("x", x_scales)
        grb_t = load_list("grb", grb)
        d_wd = load_words("d", d_words)
        load_scales(nc.sync, d_sc, d_scales, 0)
        w3_raw = keep.tile([P, PACK, K], F32, name="w3_raw", align_bytes=64)
        for half in (slice(K // 2, K), slice(0, K // 2)):
            nc.sync.dma_start(w3_raw[:, :, half], w3.rearrange("(p j) n -> p j n", j=PACK)[:, :, half])
        u = keep.tile([P, PACK], F32, name="u")
        nc.sync.dma_start(u[:], unit.rearrange("(p t) o -> p (t o)", t=PACK))
        gra_t = load_list("gra", gra)
        w2_raw = keep.tile([P, PACK, K], F32, name="w2_raw", align_bytes=64)
        for half in (slice(K // 2, K), slice(0, K // 2)):
            nc.sync.dma_start(w2_raw[:, :, half], w2.rearrange("(p j) n -> p j n", j=PACK)[:, :, half])
        rb_t = load_list("rb", rb)
        load_scales(nc.sync, e_sc, e_scales, 4)
        e_wd = load_words("e", e_words)
        ra_t = load_list("ra", ra)
        offs_t = load_list("offs", offs)
        x_wd = load_words("x", x_words)
        load_scales(nc.sync, x_sc, x_scales, 8)
        w1_raw = load_weight("w1", w1)
        sc_t = load_list("sc", sc_)
        w4_raw = load_weight("w4", w4)

        tables = {}
        for name in ("yd", "ye", "y"):
            tables[name] = [keep.tile([P, PICKED + SPARE], F32, name="%s%d" % (name, t)) for t in range(PACK)]
            for t in range(PACK):
                nc.vector.memset(tables[name][t][:, PICKED:], 0.0)

        sign_u = keep.tile([P, PACK], F32, name="sign_u")
        abs_u = keep.tile([P, PACK], F32, name="abs_u")
        neg_abs_u = keep.tile([P, PACK], F32, name="neg_abs_u")
        nc.vector.tensor_scalar(sign_u[:], u[:], 0.0, 2.0, ALU.is_ge, ALU.mult)
        nc.vector.tensor_scalar(sign_u[:], sign_u[:], 1.0, -1.0, ALU.mult, ALU.add)
        nc.vector.tensor_tensor(abs_u[:], u[:], sign_u[:], ALU.mult)
        nc.vector.tensor_scalar(neg_abs_u[:], abs_u[:], -1.0, 0.0, ALU.mult, ALU.add)

        def round_weight(name, raw, scalar_share, by_pool):
            grouped = keep.tile([P, PACK * P * PACK], BF16, name=name + "_bf", align_bytes=64)
            dst = grouped[:].rearrange("p (h e m j) -> p h m j e", h=2, e=2, j=PACK)
            src = raw[:].rearrange("p j (m h e) -> p h m j e", h=2, e=2)
            if by_pool:
                nc.gpsimd.tensor_scalar(dst, src, 1.0, 0.0, ALU.mult, ALU.add)
                return grouped
            cut = P - scalar_share
            if cut < P:
                nc.scalar.copy(grouped[:].rearrange("p (t m j) -> p m j t", t=PACK, j=PACK)[:, cut:],
                               raw[:].rearrange("p j (m t) -> p m j t", t=PACK)[:, cut:])
            if cut > 0:
                nc.vector.tensor_copy(dst[:, :, :cut], src[:, :, :cut])
            return grouped

        def quantize(name, grouped):
            width = grouped.shape[1] // PACK
            codes = keep.tile([P, width], U32, name=name + "_codes", align_bytes=64)
            scales = keep.tile([P, width], U8, name=name + "_qs", align_bytes=64)
            nc.vector.quantize_mx(out=codes[:].bitcast(FP8X4), scales=scales[:], in_=grouped[:])
            return codes, scales

        def pick(name, src, lst, dtype):
            got = keep.tile([P, PICKED], dtype, name=name, align_bytes=64)
            nc.vector.tensor_copy(got[:], src.indirect(lst[:]))
            return got

        banks = [0]

        def new_bank():
            b = banks[0] % 8
            banks[0] = banks[0] + 1
            return psum.tile([P, BANK], F32, name="bank%d" % b)

        def first_product(name, wq, words, scales, factor):
            for t in range(PACK):
                acc = new_bank()
                cols = slice(t * P, (t + 1) * P)
                nc.tensor.matmul_mx(out=acc[:], lhsT=wq[0][:, cols].bitcast(FP8X4), lhsT_scale=wq[1][:, cols],
                                    rhs=words[:].bitcast(FP8X4), rhs_scale=scales, start=True, stop=True)
                nc.scalar.activation(tables[name][t][:, :PICKED], acc[:], COPY, scale=factor[:, t : t + 1])

        lists = {"yd": rb_t, "ye": ra_t, "y": sc_t}
        fetched = {}

        def fetch(name, c, h):
            r0, n = CHUNKS[c]
            if ("sides", c) in HOME and (name, c, h) not in HOME:
                if c not in fetched:
                    fetched[c] = keep.tile([P, 4, 2, n], F32, name="sides_c%d" % c, tag=HOME["sides", c], align_bytes=64)
                got = fetched[c][:, 2 * h + (name == "ye")]
            else:
                got = keep.tile([P, 2, n], F32, name="%s_c%d%d" % (name, c, h),
                                tag=HOME.get((name, c, h), "%s_c%d%d" % (name, c, h)), align_bytes=64)[:]
            for t in (2 * h, 2 * h + 1):
                window = tables[name][t][:].indirect(lists[name][:, r0 // 16 : (r0 + n) // 16])
                if (name, c, t) in BY_VECTOR:
                    nc.vector.tensor_copy(got[:, t % 2, :], window)
                else:
                    nc.scalar.activation(got[:, t % 2, :], window, COPY)
            fetched[name, c, h] = got

        def fetch_scaffold(c):
            r0, n = CHUNKS[c]
            got = keep.tile([P, PACK, n], F32, name="s_c%d" % c, tag=HOME.get(("y", c), "s_c%d" % c), align_bytes=64)
            for t in range(PACK):
                window = tables["y"][t][:].indirect(sc_t[:, r0 // 16 : (r0 + n) // 16])
                if ("y", c, t) in BY_VECTOR:
                    nc.vector.tensor_copy(got[:, t, :], window)
                else:
                    nc.scalar.activation(got[:, t, :], window, COPY)
            return got

        def flat(ap):
            return ap.rearrange("p t n -> p (t n)")

        def side_part(c):
            pair = keep.tile([P, 2, PACK, CHUNKS[c][1]], F32, name="work_c%d" % c, tag="w1_bf", align_bytes=64)
            work, other = pair[:, 0], pair[:, 1]
            parts = [(flat(work[:, 2 * h : 2 * h + 2, :]), flat(fetched["ye", c, h]), flat(fetched["yd", c, h])) for h in range(2)]
            for h, (w, a, nb) in enumerate(parts):
                o = flat(other[:, 2 * h : 2 * h + 2, :])
                nc.vector.scalar_tensor_tensor(w, nb, 0.3, a, ALU.mult, ALU.add)
                nc.vector.scalar_tensor_tensor(o, a, 0.3, nb, ALU.mult, ALU.add)
                nc.vector.scalar_tensor_tensor(w, o, -1.0, w, ALU.mult, ALU.max)
            return work

        def add_scaffold(work, s):
            for t in range(PACK):
                nc.vector.scalar_tensor_tensor(work[:, t, :], s[:, t, :], u[:, t : t + 1], work[:, t, :], ALU.mult, ALU.add)

        def hidden(i, work, s):
            c, r0, n = PIECES[i]
            cols = slice(r0 - CHUNKS[c][0], r0 - CHUNKS[c][0] + n)
            hid = keep.tile([P, n * PACK], BF16, name="hid_%d" % i, align_bytes=64)
            nc.vector.tensor_tensor(hid[:].rearrange("p (c e t) -> p c t e", t=PACK, e=2),
                                    work[:, :, cols].rearrange("p t (c e) -> p c t e", e=2),
                                    s[:, :, cols].rearrange("p t (c e) -> p c t e", e=2), ALU.mult)
            return hid

        out_codes = keep.tile([P, MOLECULES], U32, name="out_codes", align_bytes=64)
        out_scales = keep.tile([P, MOLECULES], U8, name="out_scales", align_bytes=64)
        out_rows = out_0.rearrange("(p t) r -> p t r", t=PACK)
        out_words = out_1[0].rearrange("p n r -> p (n r)").bitcast(I32)

        def last_product(i, hq, w4q, engines):
            r0, n = PIECES[i][1:]
            res = keep.tile([P, PACK, n], F32, name="res_%d" % i)
            per_bank = BANK // n
            for t0 in range(0, PACK, per_bank):
                acc = new_bank()
                for t in range(t0, t0 + per_bank):
                    cols = slice(t * P, (t + 1) * P)
                    nc.tensor.matmul_mx(out=acc[:, (t - t0) * n : (t - t0 + 1) * n], lhsT=w4q[0][:, cols].bitcast(FP8X4),
                                        lhsT_scale=w4q[1][:, cols], rhs=hq[0][:].bitcast(FP8X4), rhs_scale=hq[1][:],
                                        start=True, stop=True)
                out_copy = nc.vector.tensor_copy if engines[t0 // per_bank] == "V" else nc.scalar.copy
                out_copy(flat(res[:, t0 : t0 + per_bank, :]), acc[:])
                nc.sync.dma_start(out_rows[:, t0 : t0 + per_bank, r0 : r0 + n], res[:, t0 : t0 + per_bank, :])
            return res

        def planes(i, res, engine):
            r0, n = PIECES[i][1:]
            rounded = keep.tile([P, n * PACK], BF16, name="rounded_%d" % i, tag=HOME.get(("rounded", i), "rounded_%d" % i), align_bytes=64)
            round_copy = nc.vector.tensor_copy if engine == "V" else nc.scalar.copy
            round_copy(rounded[:].rearrange("p (c e t) -> p c t e", t=PACK, e=2), res[:].rearrange("p t (c e) -> p c t e", e=2))
            nc.vector.quantize_mx(out=out_codes[:, r0 : r0 + n].bitcast(FP8X4), scales=out_scales[:, r0 : r0 + n], in_=rounded[:])
            nc.sync.dma_start(out_words[:, r0 : r0 + n], out_codes[:, r0 : r0 + n].bitcast(I32))

        d_w = pick("d_pw", d_wd[:].bitcast(U32), grb_t, U32)
        d_s = pick("d_ps", d_sc[:], grb_t, U8)
        w3q = quantize("w3", round_weight("w3", w3_raw, 64, False))
        first_product("yd", w3q, d_w, d_s[:], neg_abs_u)
        e_s = pick("e_ps", e_sc[:], gra_t, U8)
        w2_bf = round_weight("w2", w2_raw, 64, False)
        e_w = pick("e_pw", e_wd[:].bitcast(U32), gra_t, U32)
        w2q = quantize("w2", w2_bf)
        first_product("ye", w2q, e_w, e_s[4:P, :], abs_u)
        x_w = pick("x_pw", x_wd[:].bitcast(U32), offs_t, U32)
        x_s = pick("x_ps", x_sc[:], offs_t, U8)
        w1_bf = round_weight("w1", w1_raw, 0, False)
        w1q = quantize("w1", w1_bf)
        for h in range(2):
            fetch("yd", 0, h)
            fetch("ye", 0, h)
        first_product("y", w1q, x_w, x_s[8:P, :], sign_u)
        w4q = quantize("w4", round_weight("w4", w4_raw, 0, False))
        work = side_part(0)
        waiting = []
        for c in range(len(CHUNKS)):
            s = fetch_scaffold(c)
            if c + 1 < len(CHUNKS):
                for h in range(2):
                    fetch("yd", c + 1, h)
                    fetch("ye", c + 1, h)
            add_scaffold(work, s)
            done = []
            for i in range(len(PIECES)):
                if PIECES[i][0] == c:
                    done.append((i, last_product(i, quantize("hid%d" % i, hidden(i, work, s)), w4q, ("SSSS", "SS", "SS", "SS")[i])))
            waiting = waiting + done
            if c + 1 < len(CHUNKS):
                work = side_part(c + 1)
        for i, res in waiting:
            planes(i, res, "VVV"[i])
        for r in range(4):
            eng = nc.sync if r % 2 == 0 else nc.scalar
            eng.dma_start(out_2[0, r:16:4, :].bitcast(I32), out_scales[r:P:32, :].bitcast(I32))
